import numpy as np
import ml_dtypes


def mxq(x, axis, fmt="e4m3"):
    dtype, down = {"e4m3": (ml_dtypes.float8_e4m3fn, 7), "e5m2": (ml_dtypes.float8_e5m2, 14)}[fmt]
    v = np.moveaxis(np.asarray(x, np.float32).astype(ml_dtypes.bfloat16).astype(np.float64), axis, -1)
    blocks = v.reshape(v.shape[:-1] + (-1, 32))
    amax = np.abs(blocks).max(-1, keepdims=True)
    byte = np.maximum(np.where(amax > 0, np.frexp(amax)[1] - 1 + 127, 0) - down, 1)
    scale = np.exp2(byte - 127.0)
    codes = (blocks / scale).astype(np.float32).astype(dtype).astype(np.float64)
    return np.moveaxis((codes * scale).reshape(v.shape), -1, axis)


WIDE = False


def mx_kscale(k):
    if not WIDE:
        return np.ones(k)
    levels = np.array([10, -10, 5, -5, 0])
    if k % 512:
        return np.exp2(np.random.permutation(np.resize(levels, k // 32))).repeat(32)
    a = np.empty((k // 512, 16))
    for p in range(k // 512):
        a[p, :8] = np.random.permutation(np.resize(levels, 8))
        for g in range(8):
            far = levels[np.abs(levels - a[p, g]) >= 10]
            a[p, g + 8] = far[np.random.randint(len(far))]
    return np.exp2(a.ravel()).repeat(32)


BF16 = ml_dtypes.bfloat16


def bf(x):
    return np.asarray(x, np.float32).astype(BF16)


def f64(x):
    return np.asarray(x).astype(np.float64)


V, H, B = 1024, 2048, 1024


def draw0():
    s, t = mx_kscale(V), mx_kscale(H)
    v = np.random.standard_normal((V, B)) * s[:, None]
    w = np.random.standard_normal((H, V)) / np.sqrt(V) / s * t[:, None]
    beta = (1 + 0.1 * np.random.standard_normal((H, 1))) / t[:, None]
    return {"v": bf(v), "w": bf(w), "beta": bf(beta)}


def core(v, w, beta):
    weights = f64(w)
    scale = f64(beta)
    a = mxq(weights, 1, "e4m3") @ mxq(f64(v), 0, "e4m3")
    h = scale * (1.0 / (1.0 + np.exp(-scale * a)))
    recon = mxq(weights, 0, "e4m3").T @ mxq(h, 0, "e4m3")
    return recon


def e4m3fn_bytes(y):
    return np.clip(np.asarray(y, np.float64), -448.0, 448.0).astype(np.float32).astype(ml_dtypes.float8_e4m3fn).view(np.uint8)


def e4m3fn_values(b):
    return np.asarray(b, np.uint8).view(ml_dtypes.float8_e4m3fn).astype(np.float64)


def setup_inputs():
    d = draw0()
    x0 = np.asarray(d['v']).astype(np.float64)
    s = (np.max(np.abs(x0), axis=(1,), keepdims=True) / 448.0).astype(np.float32)
    out = {}
    for k, v in d.items():
        if k == 'v':
            out['v_bytes'] = e4m3fn_bytes(x0 / s.astype(np.float64))
            out['v_scale'] = s
        else:
            out[k] = v
    return out


def reference(v_bytes, v_scale, w, beta):
    return core(e4m3fn_values(v_bytes) * v_scale.astype(np.float64), w, beta)

@@ -1,0 +1,242 @@
+from contextlib import ExitStack
+
+import concourse.mybir as mybir
+from concourse.masks import make_identity
+
+V, H, B = 1024, 2048, 1024
+FLOPS = 2 * 2 * H * V * B
+
+F32 = mybir.dt.float32
+BF16 = mybir.dt.bfloat16
+U32 = mybir.dt.uint32
+U8 = mybir.dt.uint8
+FP8 = mybir.dt.float8_e4m3fn
+FP8X4 = mybir.dt.float8_e4m3fn_x4
+ACT = mybir.ActivationFunctionType
+ALU = mybir.AluOpType
+
+P = 128
+T = 4
+KP = P * T
+NV = V // KP
+NH = H // KP
+HALF = 512
+NB = B // HALF
+NM = V // P
+
+ORDER = (
+    "wid000V wid010S wid001V wid011S wid002V wid003V wid012S vi00V "
+    "T000P wid013S T010P E000S vi01V E010S wid110S I010P "
+    "d00V wid111S I011P wid112S T100P wid113S T110P vq01V "
+    "E100S I110P wid100V wid101V I111P E110S wid102V T101P "
+    "Y110S wid103V vq00V T111P Y111S vi10V I200P E101S "
+    "I201P Y200S I210P q110V Y201S I211P vq10V E111S "
+    "I310P d30V Y010S I311P Y310S T300P Y311S T301P "
+    "q111V T310P E300S q230V M010P E301S E310V M011P "
+    "F010S q130V M012P F011S d10V M013P F012S T311P "
+    "F013S T200P q220V E311S T201P q210V E200S T210P "
+    "q131V E201S T001P vi11V E210S T211P M030P E001S "
+    "M031P E211S q120V M032P F030S q100V M033P F031S "
+    "q121V T011P F032S vq11V M020P E011S q200V M021P "
+    "F033S M110P q101V F020S M111P X03V F021S M112P "
+    "Y011S M113P M022P Y210S M023P Y211S q201V M000P "
+    "F022S hq03V M001P F000S X01V M002P F001S M003P "
+    "F002S M100P F003S M101P F023S M102P X00V F110S "
+    "M103P F111S M120P F112S M121P F120S hq01V M122P "
+    "F121S M123P hq00V F122S M130P q221V F123S N060P "
+    "q211V F130S N040P X02V N061P F113S N041P N070P "
+    "F100S N071P M131P F101S M132P F131S X11V M133P "
+    "F132S N050P N051P F133S N030P N031P F102S N000P "
+    "N001P F103S hq02V N020P N021P hq11V N010P N062P "
+    "N042P X10V N072P N052P N032P N033P N002P J03S "
+    "N003P N022P J00S N023P q231V N011P J02S N012P "
+    "hq10V N013P N063P J01S N043P X12V N160P J04S "
+    "N161P N110P N111P N150P N151P N073P N120P J07S "
+    "J06V N121P N053P hq12V N130P J05S N131P N100P "
+    "X13V N162P N112P N152P N122P N132P N101P N102P "
+    "N170P N171P hq13V N172P N140P N141P N163P N113P "
+    "J16S N153P J11V N123P J15S N133P J12V N103P "
+    "N173P J10S J13V N142P N143P J17V J14S "
+)
+
+
+def tile_rbm_mean_field_reconstruction_s7_kernel(tc, v_bytes, v_scale, w, beta, out):
+    nc = tc.nc
+    with ExitStack() as ctx:
+        keep = ctx.enter_context(tc.tile_pool(name="keep", bufs=1))
+        rot = ctx.enter_context(tc.tile_pool(name="rot", bufs=3))
+        psum = ctx.enter_context(tc.psum_pool(name="psum", bufs=8))
+
+        v_raw = [keep.tile([P, T, B], U8, name="v_raw%d" % c, align_bytes=64) for c in range(NV)]
+        w_sb = [keep.tile([P, T, V], BF16, name="w_sb%d" % g, align_bytes=64) for g in range(NH)]
+        vs = keep.tile([P, NV, T], F32, name="vs")
+        beta_bf = keep.tile([P, NH, T], BF16, name="beta_bf")
+        beta32 = keep.tile([P, NH, T], F32, name="beta32")
+        w_view = w.rearrange("(g p t) v -> g p t v", p=P, t=T)
+        v_view = v_bytes.rearrange("(c p t) n -> c p t n", p=P, t=T)
+
+        def load_w(g, a):
+            nc.sync.dma_start(out=w_sb[g][:, 2 * a : 2 * a + 2, :], in_=w_view[g][:, 2 * a : 2 * a + 2, :])
+
+        nc.scalar.dma_start(out=vs[:], in_=v_scale.rearrange("(c p t) o -> p c (t o)", p=P, t=T))
+        nc.scalar.dma_start(out=beta_bf[:], in_=beta.rearrange("(g p t) o -> p g (t o)", p=P, t=T))
+        nc.sync.dma_start(out=v_raw[0][:, 0:2, :], in_=v_view[0][:, 0:2, :])
+        nc.sync.dma_start(out=v_raw[0][:, 2:4, :], in_=v_view[0][:, 2:4, :])
+        load_w(0, 0)
+        nc.sync.dma_start(out=v_raw[1][:], in_=v_view[1])
+        load_w(0, 1)
+        load_w(1, 0)
+        load_w(1, 1)
+        load_w(2, 0)
+        load_w(2, 1)
+        load_w(3, 0)
+        load_w(3, 1)
+
+        ident = keep.tile([P, P], F32, name="ident")
+        make_identity(nc, ident[:])
+        ident_bf = keep.tile([P, P], BF16, name="ident_bf")
+        nc.gpsimd.tensor_copy(out=ident_bf[:], in_=ident[:])
+        dummy = keep.tile([P, 1], F32, name="dummy")
+        nc.vector.memset(dummy[:], 0.0)
+        nc.scalar.activation(out=dummy[:], in_=dummy[:], func=ACT.Sigmoid)
+        nc.gpsimd.tensor_copy(out=beta32[:], in_=beta_bf[:])
+
+        v_codes = keep.tile([P, NV, B], U32, name="v_codes", align_bytes=64)
+        v_sc = keep.tile([P, NV, B], U8, name="v_sc", align_bytes=64)
+        wt_codes = keep.tile([P, NV, H], U32, name="wt_codes", align_bytes=64)
+        wt_sc = keep.tile([P, NV, H], U8, name="wt_sc", align_bytes=64)
+        w2_codes = keep.tile([P, NH, V], U32, name="w2_codes", align_bytes=64)
+        w2_sc = keep.tile([P, NH, V], U8, name="w2_sc", align_bytes=64)
+        h_codes = keep.tile([P, NH, B], U32, name="h_codes", align_bytes=64)
+        h_sc = keep.tile([P, NH, B], U8, name="h_sc", align_bytes=64)
+
+        def interleave(eng, dst, src):
+            o = dst.rearrange("p (c i) t -> p c t i", i=4)
+            s = src.rearrange("p t (c i) -> p c t i", i=4)
+            eng(out=o, in_=s)
+
+        live = {}
+
+        def cols_of(n):
+            return slice(n * HALF, (n + 1) * HALF)
+
+        def step(name, e):
+            k = name[0]
+            if name[:3] == "wid":
+                c, n, t = int(name[3]), int(name[4]), int(name[5])
+                if ("vf", c, n) not in live:
+                    v_flat = rot.tile([P, T, HALF], BF16, name="v_flat", tag="stage", align_bytes=64, bufs=14)
+                    live["vf", c, n] = v_flat
+                flat = live["vf", c, n]
+                src = v_raw[c][:, t, cols_of(n)].bitcast(FP8)
+                if e == "V":
+                    nc.vector.tensor_scalar(out=flat[:, t, :], in0=src, scalar1=vs[:, c, t : t + 1], scalar2=None, op0=ALU.mult)
+                else:
+                    nc.scalar.activation(out=flat[:, t, :], in_=src, func=ACT.Copy, scale=vs[:, c, t : t + 1])
+            elif name[:2] == "vi":
+                c, n = int(name[2]), int(name[3])
+                v_grp = rot.tile([P, HALF, T], BF16, name="v_grp", tag="stage", align_bytes=64, bufs=14)
+                live["vg", c, n] = v_grp
+                interleave(nc.vector.tensor_copy, v_grp[:], live["vf", c, n][:])
+            elif name[:2] == "vq":
+                c, n = int(name[2]), int(name[3])
+                nc.vector.quantize_mx(out=v_codes[:, c, cols_of(n)].bitcast(FP8X4), scales=v_sc[:, c, cols_of(n)], in_=live["vg", c, n][:].rearrange("p n t -> p (n t)"))
+            elif k == "T":
+                g, c, a = int(name[1]), int(name[2]), int(name[3])
+                bank = psum.tile([P, 512], F32, name="bank")
+                live["tb", g, c, a] = bank
+                for b in range(2):
+                    row = w_sb[g][:, 2 * a + b, :].bitcast(F32)
+                    for u in range(2):
+                        j = (2 * b + u) * P
+                        nc.tensor.transpose(bank[:, j : j + P], row[:, 256 * c + u : 256 * (c + 1) : 2], ident[:])
+            elif k == "E":
+                g, c, a = int(name[1]), int(name[2]), int(name[3])
+                if ("wt", g, c) not in live:
+                    wt_grp = rot.tile([P, KP, T], BF16, name="wt_grp", tag="stage", align_bytes=64, bufs=14)
+                    live["wt", g, c] = wt_grp
+                words = live["wt", g, c][:].rearrange("p m t -> p (m t)").bitcast(F32).rearrange("p (t m u) -> p t m u", t=T, u=2)
+                eng = nc.vector.tensor_copy if e == "V" else nc.scalar.copy
+                eng(out=words[:, 2 * a : 2 * a + 2], in_=live["tb", g, c, a][:].rearrange("p (t u m) -> p t m u", t=2, u=2))
+            elif name[:2] == "q1":
+                g, c = int(name[2]), int(name[3])
+                cols = slice(g * KP, (g + 1) * KP)
+                nc.vector.quantize_mx(out=wt_codes[:, c, cols].bitcast(FP8X4), scales=wt_sc[:, c, cols], in_=live["wt", g, c][:].rearrange("p m t -> p (m t)"))
+            elif k == "d":
+                g, a = int(name[1]), int(name[2])
+                w2_grp = rot.tile([P, HALF, T], BF16, name="w2_grp", tag="stage", align_bytes=64, bufs=14)
+                live["w2", g, a] = w2_grp
+                interleave(nc.scalar.copy if e == "S" else nc.vector.tensor_copy, w2_grp[:], w_sb[g][:, :, cols_of(a)])
+            elif k == "I":
+                g, a, b = int(name[1]), int(name[2]), int(name[3])
+                bank = psum.tile([P, 1024], BF16, name="bank")
+                live["ib", g, a, b] = bank
+                for j in range(2):
+                    n0 = a * HALF + b * 256 + j * P
+                    nc.tensor.matmul(bank[:, j * 512 : (j + 1) * 512], lhsT=ident_bf[:], rhs=w_sb[g][:, :, n0 : n0 + P].rearrange("p t n -> p n t"), start=True, stop=True)
+            elif k == "Y":
+                g, a, b = int(name[1]), int(name[2]), int(name[3])
+                if ("w2", g, a) not in live:
+                    w2_grp = rot.tile([P, HALF, T], BF16, name="w2_grp", tag="stage", align_bytes=64, bufs=14)
+                    live["w2", g, a] = w2_grp
+                nc.scalar.copy(out=live["w2", g, a][:].rearrange("p m t -> p (m t)")[:, b * 1024 : (b + 1) * 1024], in_=live["ib", g, a, b][:])
+            elif name[:2] == "q2":
+                g, a = int(name[2]), int(name[3])
+                nc.vector.quantize_mx(out=w2_codes[:, g, cols_of(a)].bitcast(FP8X4), scales=w2_sc[:, g, cols_of(a)], in_=live["w2", g, a][:].rearrange("p m t -> p (m t)"))
+            elif k == "M":
+                n, g, t = int(name[1]), int(name[2]), int(name[3])
+                bank = psum.tile([P, 512], F32, name="bank")
+                live["mb", n, g, t] = bank
+                m = slice(g * KP + t * P, g * KP + (t + 1) * P)
+                for c in range(NV):
+                    nc.tensor.matmul_mx(out=bank[:], lhsT=wt_codes[:, c, m].bitcast(FP8X4), lhsT_scale=wt_sc[:, c, m],
+                                        rhs=v_codes[:, c, cols_of(n)].bitcast(FP8X4), rhs_scale=v_sc[:, c, cols_of(n)],
+                                        start=(c == 0), stop=(c == NV - 1))
+            elif k == "F":
+                n, g, t = int(name[1]), int(name[2]), int(name[3])
+                if ("sig", n, g) not in live:
+                    sig = rot.tile([P, T, HALF], F32, name="sig", align_bytes=64, bufs=5)
+                    live["sig", n, g] = sig
+                nc.scalar.activation(out=live["sig", n, g][:, t, :], in_=live["mb", n, g, t][:], func=ACT.Sigmoid, scale=beta32[:, g, t : t + 1])
+            elif k == "G":
+                n, g, t = int(name[1]), int(name[2]), int(name[3])
+                if ("hf", n, g) not in live:
+                    h_flat = rot.tile([P, T, HALF], BF16, name="h_flat", tag="stage", align_bytes=64, bufs=14)
+                    live["hf", n, g] = h_flat
+                nc.scalar.activation(out=live["hf", n, g][:, t, :], in_=live["sig", n, g][:, t, :], func=ACT.Copy, scale=beta32[:, g, t : t + 1])
+            elif k == "X" and ("hf", int(name[1]), int(name[2])) in live:
+                n, g = int(name[1]), int(name[2])
+                h_grp = rot.tile([P, HALF, T], BF16, name="h_grp", tag="stage", align_bytes=64, bufs=14)
+                live["h", n, g] = h_grp
+                interleave(nc.vector.tensor_copy, h_grp[:], live["hf", n, g][:])
+            elif k == "X":
+                n, g = int(name[1]), int(name[2])
+                h_grp = rot.tile([P, HALF, T], BF16, name="h_grp", tag="stage", align_bytes=64, bufs=14)
+                live["h", n, g] = h_grp
+                nc.vector.tensor_tensor(
+                    out=h_grp[:].rearrange("p (c i) t -> p c t i", i=4),
+                    in0=live["sig", n, g][:].rearrange("p t (c i) -> p c t i", i=4),
+                    in1=beta32[:, g, :].unsqueeze(1).unsqueeze(3).to_broadcast([P, HALF // 4, T, 4]),
+                    op=ALU.mult)
+            elif name[:2] == "hq":
+                n, g = int(name[2]), int(name[3])
+                nc.vector.quantize_mx(out=h_codes[:, g, cols_of(n)].bitcast(FP8X4), scales=h_sc[:, g, cols_of(n)], in_=live["h", n, g][:].rearrange("p n t -> p (n t)"))
+            elif k == "N":
+                n, m, g = int(name[1]), int(name[2]), int(name[3])
+                if g == 0:
+                    bank = psum.tile([P, 512], F32, name="bank")
+                    live["nb", n, m] = bank
+                mc = slice(m * P, (m + 1) * P)
+                nc.tensor.matmul_mx(out=live["nb", n, m][:], lhsT=w2_codes[:, g, mc].bitcast(FP8X4), lhsT_scale=w2_sc[:, g, mc],
+                                    rhs=h_codes[:, g, cols_of(n)].bitcast(FP8X4), rhs_scale=h_sc[:, g, cols_of(n)],
+                                    start=(g == 0), stop=(g == NH - 1))
+            elif k == "J":
+                n, m = int(name[1]), int(name[2])
+                res = rot.tile([P, HALF], F32, name="res", bufs=8)
+                eng = nc.vector.tensor_copy if e == "V" else nc.scalar.copy
+                eng(out=res[:], in_=live["nb", n, m][:])
+                nc.sync.dma_start(out=out[m * P : (m + 1) * P, cols_of(n)], in_=res[:])
+
+        with tc.manual_schedule():
+            for item in ORDER.split():
+                step(item[:-1], item[-1])

@@ -25,38 +25,37 @@ NB = B // HALF
 NM = V // P
 
 ORDER = (
-    "wid000V wid010S wid001V wid011S wid002V wid003V wid012S vi00V "
-    "T000P wid013S T010P E000S vi01V E010S wid110S I010P "
-    "d00V wid111S I011P wid112S T100P wid113S T110P vq01V "
-    "E100S I110P wid100V wid101V I111P E110S wid102V T101P "
-    "Y110S wid103V vq00V T111P Y111S vi10V I200P E101S "
-    "I201P Y200S I210P q110V Y201S I211P vq10V E111S "
-    "I310P d30V Y010S I311P Y310S T300P Y311S T301P "
-    "q111V T310P E300S q230V M010P E301S E310V M011P "
-    "F010S q130V M012P F011S d10V M013P F012S T311P "
-    "F013S T200P q220V E311S T201P q210V E200S T210P "
-    "q131V E201S T001P vi11V E210S T211P M030P E001S "
-    "M031P E211S q120V M032P F030S q100V M033P F031S "
-    "q121V T011P F032S vq11V M020P E011S q200V M021P "
-    "F033S M110P q101V F020S M111P X03V F021S M112P "
-    "Y011S M113P M022P Y210S M023P Y211S q201V M000P "
-    "F022S hq03V M001P F000S X01V M002P F001S M003P "
-    "F002S M100P F003S M101P F023S M102P X00V F110S "
-    "M103P F111S M120P F112S M121P F120S hq01V M122P "
-    "F121S M123P hq00V F122S M130P q221V F123S N060P "
-    "q211V F130S N040P X02V N061P F113S N041P N070P "
-    "F100S N071P M131P F101S M132P F131S X11V M133P "
-    "F132S N050P N051P F133S N030P N031P F102S N000P "
-    "N001P F103S hq02V N020P N021P hq11V N010P N062P "
-    "N042P X10V N072P N052P N032P N033P N002P J03S "
-    "N003P N022P J00S N023P q231V N011P J02S N012P "
-    "hq10V N013P N063P J01S N043P X12V N160P J04S "
-    "N161P N110P N111P N150P N151P N073P N120P J07S "
-    "J06V N121P N053P hq12V N130P J05S N131P N100P "
-    "X13V N162P N112P N152P N122P N132P N101P N102P "
-    "N170P N171P hq13V N172P N140P N141P N163P N113P "
-    "J16S N153P J11V N123P J15S N133P J12V N103P "
-    "N173P J10S J13V N142P N143P J17V J14S "
+    "T000P wid000S wid001S wid002S wid003S wid110S wid111S wid112S "
+    "wid113S wid010V wid011V wid012V wid013V vi01V vi00V wid100V "
+    "wid101V wid102V wid103V d00V vi11V vq00V T001P T010P "
+    "E010S T011P E011S E000S E001S d01S q101V d10V "
+    "q200V d21V vi10V T100P T101P T200P T201P T110P "
+    "E110S T111P E111S E200S E201S q120V vq10V T310P "
+    "T311P T300P E300S T301P E301S E100S E101S d11S "
+    "E310S E311S q130V q111V vq01V vq11V q110V d30V "
+    "q131V q210V q100V d20V q221V T210P E210S T211P "
+    "E211S q121V q201V M010P F010S M011P F011S M012P "
+    "F012S M013P F013S X01V M030P F030S M031P F031S "
+    "M032P F032S M033P F033S X03V M000P F000S M001P "
+    "F001S M002P F002S M003P F003S X00V q211V M020P "
+    "F020S M021P F021S M022P F022S M023P F023S X02V "
+    "hq01V hq00V hq03V M110P F110S M111P F111S M112P "
+    "F112S M113P F113S d31S q231V hq02V q230V q220V "
+    "M100P F100S M101P F101S M102P F102S M103P F103S "
+    "X10V X11V hq10V M120P M121P M122P M123P M130P "
+    "F130S M131P F131S M132P F132S M133P F133S F120S "
+    "F121S F122S F123S G120S G121S G122S G123S X12V "
+    "hq11V hq12V X13V hq13V N060P N061P N062P N063P "
+    "N050P N051P N052P N053P J05S J06S N000P N001P "
+    "N002P N003P N010P N011P N012P N013P J01S N040P "
+    "N041P N042P N043P N020P N021P N022P N023P N030P "
+    "N031P N032P N033P N070P N071P N072P N073P J07S "
+    "J02S J03S J04S N100P N101P N102P N170P N171P "
+    "N172P N140P N141P N142P N160P N161P N162P N130P "
+    "N131P N132P N133P J13S N143P J14S N173P J17S "
+    "N163P J16S N103P J10S J00S N120P N121P N122P "
+    "N150P N151P N152P N123P J12S N153P J15V N110P "
+    "N111P N112P N113P J11S "
 )
 
 
@@ -79,7 +78,6 @@ def tile_rbm_mean_field_reconstruction_s7_kernel(tc, v_bytes, v_scale, w, beta, 
             nc.sync.dma_start(out=w_sb[g][:, 2 * a : 2 * a + 2, :], in_=w_view[g][:, 2 * a : 2 * a + 2, :])
 
         nc.scalar.dma_start(out=vs[:], in_=v_scale.rearrange("(c p t) o -> p c (t o)", p=P, t=T))
-        nc.scalar.dma_start(out=beta_bf[:], in_=beta.rearrange("(g p t) o -> p g (t o)", p=P, t=T))
         nc.sync.dma_start(out=v_raw[0][:, 0:2, :], in_=v_view[0][:, 0:2, :])
         nc.sync.dma_start(out=v_raw[0][:, 2:4, :], in_=v_view[0][:, 2:4, :])
         load_w(0, 0)
@@ -87,6 +85,7 @@ def tile_rbm_mean_field_reconstruction_s7_kernel(tc, v_bytes, v_scale, w, beta, 
         load_w(0, 1)
         load_w(1, 0)
         load_w(1, 1)
+        nc.sync.dma_start(out=beta_bf[:], in_=beta.rearrange("(g p t) o -> p g (t o)", p=P, t=T))
         load_w(2, 0)
         load_w(2, 1)
         load_w(3, 0)
@@ -94,8 +93,6 @@ def tile_rbm_mean_field_reconstruction_s7_kernel(tc, v_bytes, v_scale, w, beta, 
 
         ident = keep.tile([P, P], F32, name="ident")
         make_identity(nc, ident[:])
-        ident_bf = keep.tile([P, P], BF16, name="ident_bf")
-        nc.gpsimd.tensor_copy(out=ident_bf[:], in_=ident[:])
         dummy = keep.tile([P, 1], F32, name="dummy")
         nc.vector.memset(dummy[:], 0.0)
         nc.scalar.activation(out=dummy[:], in_=dummy[:], func=ACT.Sigmoid)
@@ -167,19 +164,6 @@ def tile_rbm_mean_field_reconstruction_s7_kernel(tc, v_bytes, v_scale, w, beta, 
                 w2_grp = rot.tile([P, HALF, T], BF16, name="w2_grp", tag="stage", align_bytes=64, bufs=14)
                 live["w2", g, a] = w2_grp
                 interleave(nc.scalar.copy if e == "S" else nc.vector.tensor_copy, w2_grp[:], w_sb[g][:, :, cols_of(a)])
-            elif k == "I":
-                g, a, b = int(name[1]), int(name[2]), int(name[3])
-                bank = psum.tile([P, 1024], BF16, name="bank")
-                live["ib", g, a, b] = bank
-                for j in range(2):
-                    n0 = a * HALF + b * 256 + j * P
-                    nc.tensor.matmul(bank[:, j * 512 : (j + 1) * 512], lhsT=ident_bf[:], rhs=w_sb[g][:, :, n0 : n0 + P].rearrange("p t n -> p n t"), start=True, stop=True)
-            elif k == "Y":
-                g, a, b = int(name[1]), int(name[2]), int(name[3])
-                if ("w2", g, a) not in live:
-                    w2_grp = rot.tile([P, HALF, T], BF16, name="w2_grp", tag="stage", align_bytes=64, bufs=14)
-                    live["w2", g, a] = w2_grp
-                nc.scalar.copy(out=live["w2", g, a][:].rearrange("p m t -> p (m t)")[:, b * 1024 : (b + 1) * 1024], in_=live["ib", g, a, b][:])
             elif name[:2] == "q2":
                 g, a = int(name[2]), int(name[3])
                 nc.vector.quantize_mx(out=w2_codes[:, g, cols_of(a)].bitcast(FP8X4), scales=w2_sc[:, g, cols_of(a)], in_=live["w2", g, a][:].rearrange("p m t -> p (m t)"))

from contextlib import ExitStack

import concourse.mybir as mybir
from concourse.masks import make_identity

V, H, B = 1024, 2048, 1024
FLOPS = 2 * 2 * H * V * B

F32 = mybir.dt.float32
BF16 = mybir.dt.bfloat16
U32 = mybir.dt.uint32
U8 = mybir.dt.uint8
FP8 = mybir.dt.float8_e4m3fn
FP8X4 = mybir.dt.float8_e4m3fn_x4
ACT = mybir.ActivationFunctionType
ALU = mybir.AluOpType

P = 128
T = 4
KP = P * T
NV = V // KP
NH = H // KP
HALF = 512
NB = B // HALF
NM = V // P

ORDER = (
    "T000P wid000S wid001S wid002S wid003S wid110S wid111S wid112S "
    "wid113S wid010V wid011V wid012V wid013V vi01V vi00V wid100V "
    "wid101V wid102V wid103V d00V vi11V vq00V T001P T010P "
    "E010S T011P E011S E000S E001S d01S q101V d10V "
    "q200V d21V vi10V T100P T101P T200P T201P T110P "
    "E110S T111P E111S E200S E201S q120V vq10V T310P "
    "T311P T300P E300S T301P E301S E100S E101S d11S "
    "E310S E311S q130V q111V vq01V vq11V q110V d30V "
    "q131V q210V q100V d20V q221V T210P E210S T211P "
    "E211S q121V q201V M010P F010S M011P F011S M012P "
    "F012S M013P F013S X01V M030P F030S M031P F031S "
    "M032P F032S M033P F033S X03V M000P F000S M001P "
    "F001S M002P F002S M003P F003S X00V q211V M020P "
    "F020S M021P F021S M022P F022S M023P F023S X02V "
    "hq01V hq00V hq03V M110P F110S M111P F111S M112P "
    "F112S M113P F113S d31S q231V hq02V q230V q220V "
    "M100P F100S M101P F101S M102P F102S M103P F103S "
    "X10V X11V hq10V M120P M121P M122P M123P M130P "
    "F130S M131P F131S M132P F132S M133P F133S F120S "
    "F121S F122S F123S G120S G121S G122S G123S X12V "
    "hq11V hq12V X13V hq13V N060P N061P N062P N063P "
    "N050P N051P N052P N053P J05S J06S N000P N001P "
    "N002P N003P N010P N011P N012P N013P J01S N040P "
    "N041P N042P N043P N020P N021P N022P N023P N030P "
    "N031P N032P N033P N070P N071P N072P N073P J07S "
    "J02S J03S J04S N100P N101P N102P N170P N171P "
    "N172P N140P N141P N142P N160P N161P N162P N130P "
    "N131P N132P N133P J13S N143P J14S N173P J17S "
    "N163P J16S N103P J10S J00S N120P N121P N122P "
    "N150P N151P N152P N123P J12S N153P J15V N110P "
    "N111P N112P N113P J11S "
)


def tile_rbm_mean_field_reconstruction_s7_kernel(tc, v_bytes, v_scale, w, beta, out):
    nc = tc.nc
    with ExitStack() as ctx:
        keep = ctx.enter_context(tc.tile_pool(name="keep", bufs=1))
        rot = ctx.enter_context(tc.tile_pool(name="rot", bufs=3))
        psum = ctx.enter_context(tc.psum_pool(name="psum", bufs=8))

        v_raw = [keep.tile([P, T, B], U8, name="v_raw%d" % c, align_bytes=64) for c in range(NV)]
        w_sb = [keep.tile([P, T, V], BF16, name="w_sb%d" % g, align_bytes=64) for g in range(NH)]
        vs = keep.tile([P, NV, T], F32, name="vs")
        beta_bf = keep.tile([P, NH, T], BF16, name="beta_bf")
        beta32 = keep.tile([P, NH, T], F32, name="beta32")
        w_view = w.rearrange("(g p t) v -> g p t v", p=P, t=T)
        v_view = v_bytes.rearrange("(c p t) n -> c p t n", p=P, t=T)

        def load_w(g, a):
            nc.sync.dma_start(out=w_sb[g][:, 2 * a : 2 * a + 2, :], in_=w_view[g][:, 2 * a : 2 * a + 2, :])

        nc.scalar.dma_start(out=vs[:], in_=v_scale.rearrange("(c p t) o -> p c (t o)", p=P, t=T))
        nc.sync.dma_start(out=v_raw[0][:, 0:2, :], in_=v_view[0][:, 0:2, :])
        nc.sync.dma_start(out=v_raw[0][:, 2:4, :], in_=v_view[0][:, 2:4, :])
        load_w(0, 0)
        nc.sync.dma_start(out=v_raw[1][:], in_=v_view[1])
        load_w(0, 1)
        load_w(1, 0)
        load_w(1, 1)
        nc.sync.dma_start(out=beta_bf[:], in_=beta.rearrange("(g p t) o -> p g (t o)", p=P, t=T))
        load_w(2, 0)
        load_w(2, 1)
        load_w(3, 0)
        load_w(3, 1)

        ident = keep.tile([P, P], F32, name="ident")
        make_identity(nc, ident[:])
        dummy = keep.tile([P, 1], F32, name="dummy")
        nc.vector.memset(dummy[:], 0.0)
        nc.scalar.activation(out=dummy[:], in_=dummy[:], func=ACT.Sigmoid)
        nc.gpsimd.tensor_copy(out=beta32[:], in_=beta_bf[:])

        v_codes = keep.tile([P, NV, B], U32, name="v_codes", align_bytes=64)
        v_sc = keep.tile([P, NV, B], U8, name="v_sc", align_bytes=64)
        wt_codes = keep.tile([P, NV, H], U32, name="wt_codes", align_bytes=64)
        wt_sc = keep.tile([P, NV, H], U8, name="wt_sc", align_bytes=64)
        w2_codes = keep.tile([P, NH, V], U32, name="w2_codes", align_bytes=64)
        w2_sc = keep.tile([P, NH, V], U8, name="w2_sc", align_bytes=64)
        h_codes = keep.tile([P, NH, B], U32, name="h_codes", align_bytes=64)
        h_sc = keep.tile([P, NH, B], U8, name="h_sc", align_bytes=64)

        def interleave(eng, dst, src):
            o = dst.rearrange("p (c i) t -> p c t i", i=4)
            s = src.rearrange("p t (c i) -> p c t i", i=4)
            eng(out=o, in_=s)

        live = {}

        def cols_of(n):
            return slice(n * HALF, (n + 1) * HALF)

        def step(name, e):
            k = name[0]
            if name[:3] == "wid":
                c, n, t = int(name[3]), int(name[4]), int(name[5])
                if ("vf", c, n) not in live:
                    v_flat = rot.tile([P, T, HALF], BF16, name="v_flat", tag="stage", align_bytes=64, bufs=14)
                    live["vf", c, n] = v_flat
                flat = live["vf", c, n]
                src = v_raw[c][:, t, cols_of(n)].bitcast(FP8)
                if e == "V":
                    nc.vector.tensor_scalar(out=flat[:, t, :], in0=src, scalar1=vs[:, c, t : t + 1], scalar2=None, op0=ALU.mult)
                else:
                    nc.scalar.activation(out=flat[:, t, :], in_=src, func=ACT.Copy, scale=vs[:, c, t : t + 1])
            elif name[:2] == "vi":
                c, n = int(name[2]), int(name[3])
                v_grp = rot.tile([P, HALF, T], BF16, name="v_grp", tag="stage", align_bytes=64, bufs=14)
                live["vg", c, n] = v_grp
                interleave(nc.vector.tensor_copy, v_grp[:], live["vf", c, n][:])
            elif name[:2] == "vq":
                c, n = int(name[2]), int(name[3])
                nc.vector.quantize_mx(out=v_codes[:, c, cols_of(n)].bitcast(FP8X4), scales=v_sc[:, c, cols_of(n)], in_=live["vg", c, n][:].rearrange("p n t -> p (n t)"))
            elif k == "T":
                g, c, a = int(name[1]), int(name[2]), int(name[3])
                bank = psum.tile([P, 512], F32, name="bank")
                live["tb", g, c, a] = bank
                for b in range(2):
                    row = w_sb[g][:, 2 * a + b, :].bitcast(F32)
                    for u in range(2):
                        j = (2 * b + u) * P
                        nc.tensor.transpose(bank[:, j : j + P], row[:, 256 * c + u : 256 * (c + 1) : 2], ident[:])
            elif k == "E":
                g, c, a = int(name[1]), int(name[2]), int(name[3])
                if ("wt", g, c) not in live:
                    wt_grp = rot.tile([P, KP, T], BF16, name="wt_grp", tag="stage", align_bytes=64, bufs=14)
                    live["wt", g, c] = wt_grp
                words = live["wt", g, c][:].rearrange("p m t -> p (m t)").bitcast(F32).rearrange("p (t m u) -> p t m u", t=T, u=2)
                eng = nc.vector.tensor_copy if e == "V" else nc.scalar.copy
                eng(out=words[:, 2 * a : 2 * a + 2], in_=live["tb", g, c, a][:].rearrange("p (t u m) -> p t m u", t=2, u=2))
            elif name[:2] == "q1":
                g, c = int(name[2]), int(name[3])
                cols = slice(g * KP, (g + 1) * KP)
                nc.vector.quantize_mx(out=wt_codes[:, c, cols].bitcast(FP8X4), scales=wt_sc[:, c, cols], in_=live["wt", g, c][:].rearrange("p m t -> p (m t)"))
            elif k == "d":
                g, a = int(name[1]), int(name[2])
                w2_grp = rot.tile([P, HALF, T], BF16, name="w2_grp", tag="stage", align_bytes=64, bufs=14)
                live["w2", g, a] = w2_grp
                interleave(nc.scalar.copy if e == "S" else nc.vector.tensor_copy, w2_grp[:], w_sb[g][:, :, cols_of(a)])
            elif name[:2] == "q2":
                g, a = int(name[2]), int(name[3])
                nc.vector.quantize_mx(out=w2_codes[:, g, cols_of(a)].bitcast(FP8X4), scales=w2_sc[:, g, cols_of(a)], in_=live["w2", g, a][:].rearrange("p m t -> p (m t)"))
            elif k == "M":
                n, g, t = int(name[1]), int(name[2]), int(name[3])
                bank = psum.tile([P, 512], F32, name="bank")
                live["mb", n, g, t] = bank
                m = slice(g * KP + t * P, g * KP + (t + 1) * P)
                for c in range(NV):
                    nc.tensor.matmul_mx(out=bank[:], lhsT=wt_codes[:, c, m].bitcast(FP8X4), lhsT_scale=wt_sc[:, c, m],
                                        rhs=v_codes[:, c, cols_of(n)].bitcast(FP8X4), rhs_scale=v_sc[:, c, cols_of(n)],
                                        start=(c == 0), stop=(c == NV - 1))
            elif k == "F":
                n, g, t = int(name[1]), int(name[2]), int(name[3])
                if ("sig", n, g) not in live:
                    sig = rot.tile([P, T, HALF], F32, name="sig", align_bytes=64, bufs=5)
                    live["sig", n, g] = sig
                nc.scalar.activation(out=live["sig", n, g][:, t, :], in_=live["mb", n, g, t][:], func=ACT.Sigmoid, scale=beta32[:, g, t : t + 1])
            elif k == "G":
                n, g, t = int(name[1]), int(name[2]), int(name[3])
                if ("hf", n, g) not in live:
                    h_flat = rot.tile([P, T, HALF], BF16, name="h_flat", tag="stage", align_bytes=64, bufs=14)
                    live["hf", n, g] = h_flat
                nc.scalar.activation(out=live["hf", n, g][:, t, :], in_=live["sig", n, g][:, t, :], func=ACT.Copy, scale=beta32[:, g, t : t + 1])
            elif k == "X" and ("hf", int(name[1]), int(name[2])) in live:
                n, g = int(name[1]), int(name[2])
                h_grp = rot.tile([P, HALF, T], BF16, name="h_grp", tag="stage", align_bytes=64, bufs=14)
                live["h", n, g] = h_grp
                interleave(nc.vector.tensor_copy, h_grp[:], live["hf", n, g][:])
            elif k == "X":
                n, g = int(name[1]), int(name[2])
                h_grp = rot.tile([P, HALF, T], BF16, name="h_grp", tag="stage", align_bytes=64, bufs=14)
                live["h", n, g] = h_grp
                nc.vector.tensor_tensor(
                    out=h_grp[:].rearrange("p (c i) t -> p c t i", i=4),
                    in0=live["sig", n, g][:].rearrange("p t (c i) -> p c t i", i=4),
                    in1=beta32[:, g, :].unsqueeze(1).unsqueeze(3).to_broadcast([P, HALF // 4, T, 4]),
                    op=ALU.mult)
            elif name[:2] == "hq":
                n, g = int(name[2]), int(name[3])
                nc.vector.quantize_mx(out=h_codes[:, g, cols_of(n)].bitcast(FP8X4), scales=h_sc[:, g, cols_of(n)], in_=live["h", n, g][:].rearrange("p n t -> p (n t)"))
            elif k == "N":
                n, m, g = int(name[1]), int(name[2]), int(name[3])
                if g == 0:
                    bank = psum.tile([P, 512], F32, name="bank")
                    live["nb", n, m] = bank
                mc = slice(m * P, (m + 1) * P)
                nc.tensor.matmul_mx(out=live["nb", n, m][:], lhsT=w2_codes[:, g, mc].bitcast(FP8X4), lhsT_scale=w2_sc[:, g, mc],
                                    rhs=h_codes[:, g, cols_of(n)].bitcast(FP8X4), rhs_scale=h_sc[:, g, cols_of(n)],
                                    start=(g == 0), stop=(g == NH - 1))
            elif k == "J":
                n, m = int(name[1]), int(name[2])
                res = rot.tile([P, HALF], F32, name="res", bufs=8)
                eng = nc.vector.tensor_copy if e == "V" else nc.scalar.copy
                eng(out=res[:], in_=live["nb", n, m][:])
                nc.sync.dma_start(out=out[m * P : (m + 1) * P, cols_of(n)], in_=res[:])

        with tc.manual_schedule():
            for item in ORDER.split():
                step(item[:-1], item[-1])
